import numpy as np
import ml_dtypes


def mxq(x, axis, fmt="e4m3"):
    dtype, down = {"e4m3": (ml_dtypes.float8_e4m3fn, 7), "e5m2": (ml_dtypes.float8_e5m2, 14)}[fmt]
    v = np.moveaxis(np.asarray(x, np.float32).astype(ml_dtypes.bfloat16).astype(np.float64), axis, -1)
    blocks = v.reshape(v.shape[:-1] + (-1, 32))
    amax = np.abs(blocks).max(-1, keepdims=True)
    byte = np.maximum(np.where(amax > 0, np.frexp(amax)[1] - 1 + 127, 0) - down, 1)
    scale = np.exp2(byte - 127.0)
    codes = (blocks / scale).astype(np.float32).astype(dtype).astype(np.float64)
    return np.moveaxis((codes * scale).reshape(v.shape), -1, axis)


WIDE = False


def mx_kscale(k):
    if not WIDE:
        return np.ones(k)
    levels = np.array([10, -10, 5, -5, 0])
    if k % 512:
        return np.exp2(np.random.permutation(np.resize(levels, k // 32))).repeat(32)
    a = np.empty((k // 512, 16))
    for p in range(k // 512):
        a[p, :8] = np.random.permutation(np.resize(levels, 8))
        for g in range(8):
            far = levels[np.abs(levels - a[p, g]) >= 10]
            a[p, g + 8] = far[np.random.randint(len(far))]
    return np.exp2(a.ravel()).repeat(32)


def f64(x):
    return np.asarray(x).astype(np.float64)


def striped(idx):
    return np.tile(np.asarray(idx).reshape(-1, 16).T, (8, 1)).astype(np.uint16)


def unstriped(offs):
    return offs[:16].T.reshape(-1).astype(np.int64)


def striped8(idx):
    return np.asarray(idx).reshape(8, -1, 16).transpose(0, 2, 1).reshape(128, -1).astype(np.uint16)


def unstriped8(offs):
    return offs.reshape(8, 16, -1).transpose(0, 2, 1).reshape(8, -1).astype(np.int64)


def pick8(x, idx, run):
    r = np.arange(len(x))
    return x[r[:, None], idx[r % (8 * run) // run]]


E2M1 = np.array([0.0, 0.5, 1.0, 1.5, 2.0, 3.0, 4.0, 6.0, -0.0, -0.5, -1.0, -1.5, -2.0, -3.0, -4.0, -6.0])


def pack_weight(w, fmt):
    k, n = w.shape
    w = f64(np.asarray(w, np.float32).astype(ml_dtypes.bfloat16)).reshape(k // 32, 32, n)
    amax = np.abs(w).max(1)
    if fmt == "e4m3":
        byte = np.frexp(amax)[1] - 1 + 127 - 7
    else:
        mant, ex = np.frexp(amax / 6.0)
        byte = np.where(mant > 0.5, ex, ex - 1) + 127
    byte = np.clip(np.where(amax > 0, byte, 1), 1, 254)
    scaled = (w * np.exp2(127.0 - byte)[:, None, :]).reshape(k, n).astype(np.float32)
    by_word = np.ascontiguousarray(scaled.reshape(k // 512, 128, 4, n).transpose(0, 1, 3, 2))
    if fmt == "e4m3":
        words = by_word.astype(ml_dtypes.float8_e4m3fn).view(np.uint8)
    else:
        c = by_word.astype(ml_dtypes.float4_e2m1fn).view(np.uint8) & 0xF
        words = (c[..., 0::2] | (c[..., 1::2] << 4)).reshape(k // 512, 128, 2 * n)
    return np.ascontiguousarray(words), np.ascontiguousarray(byte.astype(np.uint8).reshape(k // 512, 16, n))


def unpack_weight(words, scales, fmt):
    g, _, n = scales.shape
    words = np.ascontiguousarray(words).reshape(g, 128, n, -1)
    if fmt == "e4m3":
        vals = words.view(ml_dtypes.float8_e4m3fn).astype(np.float64)
    else:
        nib = np.empty((g, 128, n, 4), np.uint8)
        nib[..., 0::2] = words & 0xF
        nib[..., 1::2] = words >> 4
        vals = E2M1[nib]
    vals = vals * np.repeat(np.exp2(scales.astype(np.float64) - 127.0), 8, axis=1)[..., None]
    return vals.transpose(0, 1, 3, 2).reshape(g * 512, n)


def sigmoid(v):
    return 1.0 / (1.0 + np.exp(-v))


K, R, F, T, J, M = 512, 128, 512, 2048, 512, 256


def setup_inputs():
    n = np.random.standard_normal
    idx = np.random.permutation(T)[:J]
    idx2 = np.stack([np.random.permutation(J)[:M] for _ in range(8)])
    idx3 = np.stack([np.random.permutation(J)[:M] for _ in range(8)])
    fk = mx_kscale(K)
    dtabp = pack_weight(n((K, T)) / fk[:, None], "e2m1")
    tabp = pack_weight(n((K, T)) / fk[:, None], "e2m1")
    return {
        "dtab_words": dtabp[0],
        "dtab_scales": dtabp[1],
        "tab_words": tabp[0],
        "tab_scales": tabp[1],
        "w1": (n((K, R)) * 1 / np.sqrt(K) * fk[:, None]).astype(np.float32),
        "gain": (np.random.uniform(0.5, 1.5, (R, 1))).astype(np.float32),
        "steep": (np.random.uniform(0.7, 2.5, (R, 1))).astype(np.float32),
        "og": (np.random.uniform(0.5, 2.0, (R, 1))).astype(np.float32),
        "base": (0.3 * n((R, M))).astype(np.float32),
        "offs": striped(idx),
        "offs2": striped8(idx2),
        "offs3": striped8(idx3),
    }


def reference(dtab_words, dtab_scales, tab_words, tab_scales, w1, gain, steep, og, base, offs, offs2, offs3):
    idx = unstriped(offs)
    idx2 = unstriped8(offs2)
    idx3 = unstriped8(offs3)
    dtabu = unpack_weight(dtab_words, dtab_scales, "e2m1")
    tabu = unpack_weight(tab_words, tab_scales, "e2m1")
    w1q = mxq(f64(w1), 0, "e4m3")
    tabidxg = tabu[:, idx]
    a = w1q.T @ tabidxg
    dtabidxg = dtabu[:, idx]
    ta = w1q.T @ dtabidxg
    h1 = a * f64(gain)
    gt = sigmoid((pick8(h1, idx2, 16) - pick8(h1, idx3, 16)) * f64(steep))
    xh1 = ta * f64(gain)
    xgt = (pick8(xh1, idx2, 16) - pick8(xh1, idx3, 16)) * f64(steep) * gt * (1.0 - gt)
    xu1 = pick8(xh1, idx3, 16) + (pick8(xh1, idx2, 16) - pick8(xh1, idx3, 16)) * gt + xgt * (pick8(h1, idx2, 16) - pick8(h1, idx3, 16))
    y = xu1 * f64(og) + f64(base)
    return y

@@ -1,0 +1,145 @@
+from contextlib import ExitStack
+
+import concourse.mybir as mybir
+
+K, R, T, J, M = 512, 128, 2048, 512, 256
+FLOPS = 2 * 2 * K * R * J
+
+F32 = mybir.dt.float32
+BF16 = mybir.dt.bfloat16
+I32 = mybir.dt.int32
+U32 = mybir.dt.uint32
+U16 = mybir.dt.uint16
+U8 = mybir.dt.uint8
+FP8X4 = mybir.dt.float8_e4m3fn_x4
+FP4X4 = mybir.dt.float4_e2m1fn_x4
+ALU = mybir.AluOpType
+ACT = mybir.ActivationFunctionType
+
+P = 128
+PACK = 4
+HALF_J = J // 2
+HALF_M = M // 2
+LIST_COLS = HALF_M // 16
+
+
+def tile_attend_tcsoftlarger_kernel(tc, dtab_words, dtab_scales, tab_words, tab_scales, w1, gain, steep, og, base,
+                                     offs, offs2, offs3, out):
+    nc = tc.nc
+    with ExitStack() as ctx:
+        sb = ctx.enter_context(tc.tile_pool(name="sb", bufs=1))
+        ps = ctx.enter_context(tc.psum_pool(name="ps", bufs=1))
+
+        slots = sb.tile([P, J // 16], U16, name="slots")
+        picks2 = sb.tile([P, M // 16], U16, name="picks2")
+        picks3 = sb.tile([P, M // 16], U16, name="picks3")
+        nc.sync.dma_start(slots[:], offs)
+        nc.sync.dma_start(picks3[:], offs3)
+        nc.sync.dma_start(picks2[:], offs2)
+
+        def zeroed_plane(name):
+            plane = sb.tile([P, T], U8, name=name, align_bytes=64)
+            nc.vector.memset(plane[:].bitcast(I32), 0)
+            return plane
+
+        def load_plane(plane, scales):
+            for q in range(4):
+                nc.sync.dma_start(plane[32 * q : 32 * q + 4, :].bitcast(I32), scales[0, 4 * q : 4 * q + 4, :].bitcast(I32))
+
+        def load_words(name, words):
+            tile = sb.tile([P, T], U16, name=name, align_bytes=64)
+            nc.sync.dma_start(tile[:].bitcast(I32), words[0].bitcast(I32))
+            return tile
+
+        tab_plane = zeroed_plane("tab_plane")
+        dtab_plane = zeroed_plane("dtab_plane")
+        load_plane(tab_plane, tab_scales)
+        tab_all = load_words("tab_all", tab_words)
+        w_raw = sb.tile([P, PACK, R], F32, name="w_raw")
+        nc.sync.dma_start(w_raw[:], w1.rearrange("(p t) r -> p t r", t=PACK))
+        dtab_all = load_words("dtab_all", dtab_words)
+        load_plane(dtab_plane, dtab_scales)
+        base_sb = sb.tile([P, M], F32, name="base_sb")
+        nc.sync.dma_start(base_sb[:], base)
+
+        gain_sb = sb.tile([P, 1], F32, name="gain_sb")
+        steep_sb = sb.tile([P, 1], F32, name="steep_sb")
+        og_sb = sb.tile([P, 1], F32, name="og_sb")
+        nc.gpsimd.dma_start(gain_sb[:], gain)
+        nc.gpsimd.dma_start(steep_sb[:], steep)
+        nc.gpsimd.dma_start(og_sb[:], og)
+
+        warm_in = sb.tile([P, 1], F32, name="warm_in")
+        warm_out = sb.tile([P, 1], F32, name="warm_out")
+        nc.vector.memset(warm_in[:], 0.0)
+        nc.scalar.activation(warm_out[:], warm_in[:], ACT.Silu)
+
+        half_steep = sb.tile([P, 1], F32, name="half_steep")
+        half_og = sb.tile([P, 1], F32, name="half_og")
+        minus_half_og = sb.tile([P, 1], F32, name="minus_half_og")
+        nc.gpsimd.tensor_scalar(half_steep[:], steep_sb[:], 0.5, 0.0, ALU.mult, ALU.add)
+        nc.gpsimd.tensor_scalar(half_og[:], og_sb[:], 0.5, 0.0, ALU.mult, ALU.add)
+        nc.gpsimd.tensor_scalar(minus_half_og[:], og_sb[:], -0.5, 0.0, ALU.mult, ALU.add)
+
+        def gather(name, window, dtype):
+            tile = sb.tile([P, J], dtype, name=name, align_bytes=64)
+            nc.vector.tensor_copy(tile[:], window[:].indirect(slots[:]))
+            return tile
+
+        tab_scale = gather("tab_scale", tab_plane, U8)
+        tab_code = gather("tab_code", tab_all, U16)
+
+        w_bf = sb.tile([P, R, PACK], BF16, name="w_bf", align_bytes=64)
+        nc.scalar.copy(w_bf[:], w_raw[:].rearrange("p t r -> p r t"))
+        w_code = sb.tile([P, R], U32, name="w_code", align_bytes=64)
+        w_scale = sb.tile([P, R], U8, name="w_scale", align_bytes=64)
+        nc.vector.quantize_mx(out=w_code[:].bitcast(FP8X4), scales=w_scale[:], in_=w_bf[:].rearrange("p r t -> p (r t)"))
+
+        dtab_code = gather("dtab_code", dtab_all, U16)
+        dtab_scale = gather("dtab_scale", dtab_plane, U8)
+
+        def layer(name, code, scale):
+            result = sb.tile([P, J], F32, name=name)
+            for h in range(2):
+                cols = slice(h * HALF_J, (h + 1) * HALF_J)
+                bank = ps.tile([P, HALF_J], F32, name=name + "_bank" + str(h))
+                nc.tensor.matmul_mx(out=bank[:], lhsT=w_code[:].bitcast(FP8X4), lhsT_scale=w_scale[:],
+                                    rhs=code[:, cols].bitcast(FP4X4), rhs_scale=scale[:, cols], start=True, stop=True)
+                nc.scalar.activation(result[:, cols], bank[:], ACT.Copy, scale=gain_sb[:])
+            return result
+
+        h1 = layer("h1", tab_code, tab_scale)
+        xh1 = layer("xh1", dtab_code, dtab_scale)
+
+        halves = [(slice(h * HALF_M, (h + 1) * HALF_M), slice(h * LIST_COLS, (h + 1) * LIST_COLS)) for h in range(2)]
+
+        def pick_and_subtract(name, window, first, second):
+            picked = sb.tile([P, M], F32, name=name + "_pick")
+            diff = sb.tile([P, M], F32, name=name + "_diff")
+            for cols, lcols in halves:
+                nc.vector.tensor_copy(picked[:, cols], window[:].indirect(first[:, lcols]))
+            for cols, lcols in halves:
+                nc.vector.tensor_tensor(diff[:, cols], window[:].indirect(second[:, lcols]), picked[:, cols], ALU.subtract)
+            return picked, diff
+
+        h3, d = pick_and_subtract("h", h1, picks3, picks2)
+        x2, xe = pick_and_subtract("x", xh1, picks2, picks3)
+
+        th = sb.tile([P, M], F32, name="th")
+        si = sb.tile([P, M], F32, name="si")
+        lo = sb.tile([P, M], F32, name="lo")
+        nc.scalar.activation(th[:], d[:], ACT.Tanh, scale=half_steep[:])
+        nc.scalar.activation(si[:], d[:], ACT.Silu, scale=steep_sb[:])
+        nc.scalar.activation(lo[:], th[:], ACT.Identity, scale=half_og[:], bias=minus_half_og[:])
+
+        wt = sb.tile([P, M], F32, name="wt")
+        up = sb.tile([P, M], F32, name="up")
+        tt = sb.tile([P, M], F32, name="tt")
+        res = sb.tile([P, M], F32, name="res")
+        nc.vector.scalar_tensor_tensor(wt[:], si[:], 1.0, lo[:], ALU.subtract, ALU.mult)
+        nc.vector.scalar_tensor_tensor(up[:], x2[:], og_sb[:], base_sb[:], ALU.mult, ALU.add)
+        for cols, lcols in halves:
+            nc.vector.tensor_tensor(tt[:, cols], wt[:, cols], xe[:, cols], ALU.mult)
+        for cols, lcols in halves:
+            nc.vector.tensor_tensor(res[:, cols], tt[:, cols], up[:, cols], ALU.add)
+        nc.sync.dma_start(out, res[:])

@@ -34,7 +34,6 @@ def tile_attend_tcsoftlarger_kernel(tc, dtab_words, dtab_scales, tab_words, tab_
         picks2 = sb.tile([P, M // 16], U16, name="picks2")
         picks3 = sb.tile([P, M // 16], U16, name="picks3")
         nc.sync.dma_start(slots[:], offs)
-        nc.sync.dma_start(picks3[:], offs3)
         nc.sync.dma_start(picks2[:], offs2)
 
         def zeroed_plane(name):
@@ -43,7 +42,7 @@ def tile_attend_tcsoftlarger_kernel(tc, dtab_words, dtab_scales, tab_words, tab_
             return plane
 
         def load_plane(plane, scales):
-            for q in range(4):
+            for q in (0, 2, 1, 3):
                 nc.sync.dma_start(plane[32 * q : 32 * q + 4, :].bitcast(I32), scales[0, 4 * q : 4 * q + 4, :].bitcast(I32))
 
         def load_words(name, words):
@@ -59,6 +58,7 @@ def tile_attend_tcsoftlarger_kernel(tc, dtab_words, dtab_scales, tab_words, tab_
         nc.sync.dma_start(w_raw[:], w1.rearrange("(p t) r -> p t r", t=PACK))
         dtab_all = load_words("dtab_all", dtab_words)
         load_plane(dtab_plane, dtab_scales)
+        nc.sync.dma_start(picks3[:], offs3)
         base_sb = sb.tile([P, M], F32, name="base_sb")
         nc.sync.dma_start(base_sb[:], base)
 
@@ -81,9 +81,11 @@ def tile_attend_tcsoftlarger_kernel(tc, dtab_words, dtab_scales, tab_words, tab_
         nc.gpsimd.tensor_scalar(half_og[:], og_sb[:], 0.5, 0.0, ALU.mult, ALU.add)
         nc.gpsimd.tensor_scalar(minus_half_og[:], og_sb[:], -0.5, 0.0, ALU.mult, ALU.add)
 
-        def gather(name, window, dtype):
+        def gather(name, window, dtype, pieces=1):
             tile = sb.tile([P, J], dtype, name=name, align_bytes=64)
-            nc.vector.tensor_copy(tile[:], window[:].indirect(slots[:]))
+            n = J // pieces
+            for i in range(pieces):
+                nc.vector.tensor_copy(tile[:, i * n : (i + 1) * n], window[:].indirect(slots[:, i * n // 16 : (i + 1) * n // 16]))
             return tile
 
         tab_scale = gather("tab_scale", tab_plane, U8)
@@ -96,7 +98,7 @@ def tile_attend_tcsoftlarger_kernel(tc, dtab_words, dtab_scales, tab_words, tab_
         nc.vector.quantize_mx(out=w_code[:].bitcast(FP8X4), scales=w_scale[:], in_=w_bf[:].rearrange("p r t -> p (r t)"))
 
         dtab_code = gather("dtab_code", dtab_all, U16)
-        dtab_scale = gather("dtab_scale", dtab_plane, U8)
+        dtab_scale = gather("dtab_scale", dtab_plane, U8, 2)
 
         def layer(name, code, scale):
             result = sb.tile([P, J], F32, name=name)
@@ -125,15 +127,15 @@ def tile_attend_tcsoftlarger_kernel(tc, dtab_words, dtab_scales, tab_words, tab_
         h3, d = pick_and_subtract("h", h1, picks3, picks2)
         x2, xe = pick_and_subtract("x", xh1, picks2, picks3)
 
-        th = sb.tile([P, M], F32, name="th")
+        th = sb.tile([P, M], F32, name="th", tag="th")
         si = sb.tile([P, M], F32, name="si")
         lo = sb.tile([P, M], F32, name="lo")
-        nc.scalar.activation(th[:], d[:], ACT.Tanh, scale=half_steep[:])
-        nc.scalar.activation(si[:], d[:], ACT.Silu, scale=steep_sb[:])
+        nc.scalar.activation(th[:], d[:], ACT.Tanh, scale=half_steep[:], bias=warm_out[:])
+        nc.scalar.activation(si[:], d[:], ACT.Silu, scale=steep_sb[:], bias=warm_out[:])
         nc.scalar.activation(lo[:], th[:], ACT.Identity, scale=half_og[:], bias=minus_half_og[:])
 
         wt = sb.tile([P, M], F32, name="wt")
-        up = sb.tile([P, M], F32, name="up")
+        up = sb.tile([P, M], F32, name="up", tag="th")
         tt = sb.tile([P, M], F32, name="tt")
         res = sb.tile([P, M], F32, name="res")
         nc.vector.scalar_tensor_tensor(wt[:], si[:], 1.0, lo[:], ALU.subtract, ALU.mult)

from contextlib import ExitStack

import concourse.mybir as mybir

K, R, T, J, M = 512, 128, 2048, 512, 256
FLOPS = 2 * 2 * K * R * J

F32 = mybir.dt.float32
BF16 = mybir.dt.bfloat16
I32 = mybir.dt.int32
U32 = mybir.dt.uint32
U16 = mybir.dt.uint16
U8 = mybir.dt.uint8
FP8X4 = mybir.dt.float8_e4m3fn_x4
FP4X4 = mybir.dt.float4_e2m1fn_x4
ALU = mybir.AluOpType
ACT = mybir.ActivationFunctionType

P = 128
PACK = 4
HALF_J = J // 2
HALF_M = M // 2
LIST_COLS = HALF_M // 16


def tile_attend_tcsoftlarger_kernel(tc, dtab_words, dtab_scales, tab_words, tab_scales, w1, gain, steep, og, base,
                                     offs, offs2, offs3, out):
    nc = tc.nc
    with ExitStack() as ctx:
        sb = ctx.enter_context(tc.tile_pool(name="sb", bufs=1))
        ps = ctx.enter_context(tc.psum_pool(name="ps", bufs=1))

        slots = sb.tile([P, J // 16], U16, name="slots")
        picks2 = sb.tile([P, M // 16], U16, name="picks2")
        picks3 = sb.tile([P, M // 16], U16, name="picks3")
        nc.sync.dma_start(slots[:], offs)
        nc.sync.dma_start(picks2[:], offs2)

        def zeroed_plane(name):
            plane = sb.tile([P, T], U8, name=name, align_bytes=64)
            nc.vector.memset(plane[:].bitcast(I32), 0)
            return plane

        def load_plane(plane, scales):
            for q in (0, 2, 1, 3):
                nc.sync.dma_start(plane[32 * q : 32 * q + 4, :].bitcast(I32), scales[0, 4 * q : 4 * q + 4, :].bitcast(I32))

        def load_words(name, words):
            tile = sb.tile([P, T], U16, name=name, align_bytes=64)
            nc.sync.dma_start(tile[:].bitcast(I32), words[0].bitcast(I32))
            return tile

        tab_plane = zeroed_plane("tab_plane")
        dtab_plane = zeroed_plane("dtab_plane")
        load_plane(tab_plane, tab_scales)
        tab_all = load_words("tab_all", tab_words)
        w_raw = sb.tile([P, PACK, R], F32, name="w_raw")
        nc.sync.dma_start(w_raw[:], w1.rearrange("(p t) r -> p t r", t=PACK))
        dtab_all = load_words("dtab_all", dtab_words)
        load_plane(dtab_plane, dtab_scales)
        nc.sync.dma_start(picks3[:], offs3)
        base_sb = sb.tile([P, M], F32, name="base_sb")
        nc.sync.dma_start(base_sb[:], base)

        gain_sb = sb.tile([P, 1], F32, name="gain_sb")
        steep_sb = sb.tile([P, 1], F32, name="steep_sb")
        og_sb = sb.tile([P, 1], F32, name="og_sb")
        nc.gpsimd.dma_start(gain_sb[:], gain)
        nc.gpsimd.dma_start(steep_sb[:], steep)
        nc.gpsimd.dma_start(og_sb[:], og)

        warm_in = sb.tile([P, 1], F32, name="warm_in")
        warm_out = sb.tile([P, 1], F32, name="warm_out")
        nc.vector.memset(warm_in[:], 0.0)
        nc.scalar.activation(warm_out[:], warm_in[:], ACT.Silu)

        half_steep = sb.tile([P, 1], F32, name="half_steep")
        half_og = sb.tile([P, 1], F32, name="half_og")
        minus_half_og = sb.tile([P, 1], F32, name="minus_half_og")
        nc.gpsimd.tensor_scalar(half_steep[:], steep_sb[:], 0.5, 0.0, ALU.mult, ALU.add)
        nc.gpsimd.tensor_scalar(half_og[:], og_sb[:], 0.5, 0.0, ALU.mult, ALU.add)
        nc.gpsimd.tensor_scalar(minus_half_og[:], og_sb[:], -0.5, 0.0, ALU.mult, ALU.add)

        def gather(name, window, dtype, pieces=1):
            tile = sb.tile([P, J], dtype, name=name, align_bytes=64)
            n = J // pieces
            for i in range(pieces):
                nc.vector.tensor_copy(tile[:, i * n : (i + 1) * n], window[:].indirect(slots[:, i * n // 16 : (i + 1) * n // 16]))
            return tile

        tab_scale = gather("tab_scale", tab_plane, U8)
        tab_code = gather("tab_code", tab_all, U16)

        w_bf = sb.tile([P, R, PACK], BF16, name="w_bf", align_bytes=64)
        nc.scalar.copy(w_bf[:], w_raw[:].rearrange("p t r -> p r t"))
        w_code = sb.tile([P, R], U32, name="w_code", align_bytes=64)
        w_scale = sb.tile([P, R], U8, name="w_scale", align_bytes=64)
        nc.vector.quantize_mx(out=w_code[:].bitcast(FP8X4), scales=w_scale[:], in_=w_bf[:].rearrange("p r t -> p (r t)"))

        dtab_code = gather("dtab_code", dtab_all, U16)
        dtab_scale = gather("dtab_scale", dtab_plane, U8, 2)

        def layer(name, code, scale):
            result = sb.tile([P, J], F32, name=name)
            for h in range(2):
                cols = slice(h * HALF_J, (h + 1) * HALF_J)
                bank = ps.tile([P, HALF_J], F32, name=name + "_bank" + str(h))
                nc.tensor.matmul_mx(out=bank[:], lhsT=w_code[:].bitcast(FP8X4), lhsT_scale=w_scale[:],
                                    rhs=code[:, cols].bitcast(FP4X4), rhs_scale=scale[:, cols], start=True, stop=True)
                nc.scalar.activation(result[:, cols], bank[:], ACT.Copy, scale=gain_sb[:])
            return result

        h1 = layer("h1", tab_code, tab_scale)
        xh1 = layer("xh1", dtab_code, dtab_scale)

        halves = [(slice(h * HALF_M, (h + 1) * HALF_M), slice(h * LIST_COLS, (h + 1) * LIST_COLS)) for h in range(2)]

        def pick_and_subtract(name, window, first, second):
            picked = sb.tile([P, M], F32, name=name + "_pick")
            diff = sb.tile([P, M], F32, name=name + "_diff")
            for cols, lcols in halves:
                nc.vector.tensor_copy(picked[:, cols], window[:].indirect(first[:, lcols]))
            for cols, lcols in halves:
                nc.vector.tensor_tensor(diff[:, cols], window[:].indirect(second[:, lcols]), picked[:, cols], ALU.subtract)
            return picked, diff

        h3, d = pick_and_subtract("h", h1, picks3, picks2)
        x2, xe = pick_and_subtract("x", xh1, picks2, picks3)

        th = sb.tile([P, M], F32, name="th", tag="th")
        si = sb.tile([P, M], F32, name="si")
        lo = sb.tile([P, M], F32, name="lo")
        nc.scalar.activation(th[:], d[:], ACT.Tanh, scale=half_steep[:], bias=warm_out[:])
        nc.scalar.activation(si[:], d[:], ACT.Silu, scale=steep_sb[:], bias=warm_out[:])
        nc.scalar.activation(lo[:], th[:], ACT.Identity, scale=half_og[:], bias=minus_half_og[:])

        wt = sb.tile([P, M], F32, name="wt")
        up = sb.tile([P, M], F32, name="up", tag="th")
        tt = sb.tile([P, M], F32, name="tt")
        res = sb.tile([P, M], F32, name="res")
        nc.vector.scalar_tensor_tensor(wt[:], si[:], 1.0, lo[:], ALU.subtract, ALU.mult)
        nc.vector.scalar_tensor_tensor(up[:], x2[:], og_sb[:], base_sb[:], ALU.mult, ALU.add)
        for cols, lcols in halves:
            nc.vector.tensor_tensor(tt[:, cols], wt[:, cols], xe[:, cols], ALU.mult)
        for cols, lcols in halves:
            nc.vector.tensor_tensor(res[:, cols], tt[:, cols], up[:, cols], ALU.add)
        nc.sync.dma_start(out, res[:])
